import numpy as np, ml_dtypes
CORES = [3,11,19,27,35,43,51,59]
N = 8
import mx_ref
BF = ml_dtypes.bfloat16
def cols(t, e):
    v = np.concatenate([t.reshape(128, -1, 4), np.zeros((128, 1, 4), BF)], axis=1)
    return np.ascontiguousarray(v[:, e]).reshape(128, -1)
def cut(t, i, w=512):
    return t[:, w * i:w * i + w]
def f(rng, *shape):
    return mx_ref.flush((rng.standard_normal(shape, dtype=np.float32) * np.exp2(rng.integers(-2, 3, shape[:-1] + (1,)))).astype(BF))
def wide(rng, *shape, cols=0):
    v = rng.standard_normal(shape, dtype=np.float32) * np.exp2(rng.integers(-12, 13, shape)).astype(np.float32)
    if cols: v *= np.repeat(np.exp2(rng.integers(-cols, cols + 1, shape[:-2] + (1, shape[-1] // 4))) * (rng.random(shape[:-2] + (1, shape[-1] // 4)) > 0.0625), 4, axis=-1).astype(np.float32)
    return mx_ref.flush(v.astype(BF))
T, O, CH = 512, 2, 64
def order(x, u):
    score = mx_ref.matmul(mx_ref.quantize(u), mx_ref.quantize(x))[0] + np.float32(0.0)
    return np.lexsort((np.arange(T), -score))
def held(t):
    t = t.copy(); t[np.abs(t.astype(np.float32)) < 2.0 ** -30] = 0; return t
def first(v):
    t = np.zeros((N, 128, 512), BF); t[:, :, :4] = v; return t
def setup_inputs(rng):
    return {"x": held(f(rng, N, 128, 4 * T)), "u": first(held(f(rng, N, 128, 4))), "w": held(f(rng, N, 128, O * 512))}
def setup_inputs_ties(rng):
    d = setup_inputs(rng)
    for r in range(N):
        k = N - 1 if r % 2 else T // 8
        d["x"][r] = cols(d["x"][r], rng.permutation(T)[:k][rng.integers(0, k, T)])
    return d
def setup_inputs_falling(rng):
    d = setup_inputs(rng); d["x"] = np.stack([cols(d["x"][r], order(d["x"][r], d["u"][r])) for r in range(N)]); return d
def setup_inputs_near(rng):
    d = setup_inputs(rng); k = T // 8
    for r in range(N): d["x"][r] = cols(d["x"][r], rng.permutation(T)[:k][rng.permutation(T) % k])
    d["x"][:, :8] = held((f(rng, N, 8, 4 * T).astype(np.float32) * np.float32(2.0 ** -20)).astype(BF))
    return d
def setup_inputs_zeros(rng):
    d = setup_inputs(rng); d["u"][rng.permutation(N)[:N // 2]] = 0; return d
def setup_inputs_spread(rng):
    d = setup_inputs(rng); d["x"] = held(wide(rng, N, 128, 4 * T, cols=8)); d["u"] = first(held(wide(rng, N, 128, 4))); return d
def check_inputs(d):
    b = []
    for k in ("x", "u", "w"):
        a = np.abs(d[k].astype(np.float32))
        ok = ((a == 0) | ((a >= 2.0 ** -30) & (a <= 2.0 ** 30))).all()
        if k == "u" and not (a[:, :, 4:] == 0).all(): ok = False
        if not ok: b.append(k)
    return b
def reference(x, u, w):
    y = np.zeros((N, 128, N * O * CH), np.float32); ix = np.zeros((N, N, CH), np.float32)
    W = [[mx_ref.quantize(np.ascontiguousarray(cut(w[d], o))) for o in range(O)] for d in range(N)]
    for s in range(N):
        e = order(x[s], u[s])
        for d in range(N):
            run = e[d * CH:d * CH + CH]
            ix[d, s] = run
            t = mx_ref.quantize(cols(x[s], run))
            for o in range(O):
                k = (s * O + o) * CH
                y[d][:, k:k + CH] = mx_ref.matmul(W[d][o], t)
    return {"y": y, "ix": ix}

@@ -1,0 +1,326 @@
+from concourse.bass import DstId, RemoteDMATransfer
+from concourse.mybir import AluOpType, ActivationFunctionType
+
+N, TC, O, CH = 8, 512, 2, 64
+MX4 = "float8_e4m3fn_x4"
+SCRATCH = {
+    "UB": ("sbuf", [128, 16], "bfloat16"),
+    "UR": ("sbuf", [128, 512], "bfloat16"),
+    "UQ": ("sbuf", [128, 128], MX4), "US": ("sbuf", [128, 128], "uint8"),
+    "XB": ("sbuf", [128, 2048], "bfloat16"),
+    "XQ": ("sbuf", [128, 512], MX4), "XS": ("sbuf", [128, 512], "uint8"),
+    "WB": ("sbuf", [128, 1024], "bfloat16"),
+    "WQ": ("sbuf", [128, 256], MX4), "WS": ("sbuf", [128, 256], "uint8"),
+    "PI": ("sbuf", [128, 32], "int32"),
+    "UI": ("sbuf", [128, 32], "int32"), "UO": ("sbuf", [128, 32], "uint16"),
+    "GI": ("sbuf", [128, 8], "int32"), "GF": ("sbuf", [128, 8], "float32"),
+    "JF": ("sbuf", [128, 128], "float32"), "J": ("sbuf", [128, 128], "bfloat16"),
+    "ONE": ("sbuf", [128, 128], "bfloat16"), "MK": ("sbuf", [128, 128], "bfloat16"),
+    "C": ("sbuf", [128, 2560], "bfloat16"),
+    "EQ": ("sbuf", [128, 512], "bfloat16"),
+    "JK": ("sbuf", [128, 1560], "bfloat16"),
+    "CNT": ("sbuf", [128, 264], "float32"),
+    "XM": ("sbuf", [128, 8], "float32"), "OF": ("sbuf", [128, 8], "uint16"),
+    "SW": ("sbuf", [128, 1024], "bfloat16"), "TT": ("sbuf", [128, 1024], "bfloat16"),
+    "Z": ("sbuf", [128, 128], "bfloat16"), "HA": ("sbuf", [128, 64], "bfloat16"), "HB": ("sbuf", [128, 32], "bfloat16"),
+    "OT0": ("sbuf", [128, 32], "uint16"), "OT1": ("sbuf", [128, 32], "uint16"),
+    "OT2": ("sbuf", [128, 32], "uint16"), "OT3": ("sbuf", [128, 32], "uint16"),
+    "G": ("sbuf", [128, 2048], "bfloat16"),
+    "GQ": ("sbuf", [128, 512], MX4), "GS": ("sbuf", [128, 512], "uint8"),
+    "LAQ": ("sbuf", [128, 256], MX4), "LAS": ("sbuf", [128, 256], "uint8"),
+    "LBQ": ("sbuf", [128, 192], MX4), "LBS": ("sbuf", [128, 192], "uint8"),
+    "IV": ("sbuf", [128, 32], "bfloat16"), "IF": ("sbuf", [128, 32], "float32"),
+    "IXD": ("dram", [8, 128, 1], "float32"), "IXL": ("dram", [8, 128, 1], "float32"),
+    "Y": ("sbuf", [128, 1024], "float32"),
+    "SB0": ("psum", [128, 512], "float32"), "SB1": ("psum", [128, 512], "float32"),
+    "SC0": ("psum", [128, 512], "float32"), "SC1": ("psum", [128, 512], "float32"),
+    "SC2": ("psum", [128, 512], "float32"), "SC3": ("psum", [128, 512], "float32"),
+}
+NEV = 100
+SEMAPHORES = ["arrA", "arrB", "arrX", "sent"] + ["e%d" % i for i in range(NEV)]
+MAGIC = 1.5 * 2.0 ** 27
+
+
+def rank_program(g, core, T, topo):
+    r = T.rank_of(core)
+    if r is None:
+        return
+    add, sub, mult = AluOpType.add, AluOpType.subtract, AluOpType.mult
+    ge, gt, eq = AluOpType.is_ge, AluOpType.is_gt, AluOpType.is_equal
+    Copy = ActivationFunctionType.Copy
+    v, s, te, sy = g.vector, g.scalar, g.tensor, g.sync
+    Q = {"g": g, "v": v, "s": s, "t": te, "y": sy}
+    events, seen, done = [], set(), set()
+
+    def ev():
+        h = [len(events), 0]
+        events.append(h)
+        return h
+
+    def inc(h, ins, n=1):
+        ins.then_inc(T.sem["e%d" % h[0]], n)
+        h[1] += n
+        return h
+
+    def one(ins, n=1):
+        return inc(ev(), ins, n)
+
+    def need(q, *hs):
+        for h in hs:
+            if (q, h[0]) not in seen:
+                seen.add((q, h[0]))
+                done.add(h[0])
+                Q[q].wait_ge(T.sem["e%d" % h[0]], h[1])
+
+    hx = [None] * 4
+    hu = one(sy.dma_start(T.UB[:], T.u[:, 0:16]), 16)
+    for a in range(4):
+        q = s if a % 2 == 0 else sy
+        hx[a] = one(q.dma_start(T.XB[:, 512 * a:512 * a + 512], T.x[:, 512 * a:512 * a + 512]), 16)
+    hw = one(sy.dma_start(T.WB[:], T.w[:]), 16)
+
+    hpi = one(g.iota(T.PI[:], [[0, 32]], 0, 1))
+    hjf = one(g.iota(T.JF[:], [[128, 4], [0, 2], [1, 16]], -256, 0, allow_small_or_imprecise_dtypes=True))
+    hone = one(v.memset(T.ONE[:], 1.0))
+    need("g", hone)
+    hmk = one(g.affine_select(T.MK[:], T.ONE[:], [[1, 128]], ge, 0.0, 0, -1))
+    need("v", hpi)
+    hui = one(v.tensor_scalar(T.UI[:], T.PI[:], 3, None, AluOpType.bitwise_and))
+    hgi = one(v.tensor_scalar(T.GI[:, 0:1], T.PI[:, 0:1], 112, None, AluOpType.bitwise_and))
+    need("v", hui)
+    huo = one(v.tensor_copy(T.UO[:], T.UI[:]))
+    need("v", hgi)
+    hgf = one(v.tensor_copy(T.GF[:, 0:1], T.GI[:, 0:1]))
+    need("v", huo, hu)
+    hur = one(v.tensor_copy(T.UR[:], T.UB[:, 0:16].indirect(T.UO[:, 0:32])))
+    need("v", hgf, hjf)
+    hj = one(v.tensor_scalar(T.J[:], T.JF[:], T.GF[:, 0:1], None, add))
+    need("v", hur)
+    huq = one(v.quantize_mx(T.UQ[:], T.US[:], T.UR[:]))
+    hsw = one(v.memset(T.SW[:], 0.0))
+
+    hq, hsc, hsb = [None] * 4, [None] * 4, [None] * 2
+
+    def quant_x(a):
+        need("v", hx[a])
+        hq[a] = one(v.quantize_mx(T.XQ[:, 128 * a:128 * a + 128], T.XS[:, 128 * a:128 * a + 128],
+                                  T.XB[:, 512 * a:512 * a + 512]))
+
+    def score_col(a):
+        need("t", huq, hq[a])
+        hsc[a] = one(te.matmul_mx(T["SC%d" % a][:, 0:128], T.XQ[:, 128 * a:128 * a + 128],
+                                  T.XS[:, 128 * a:128 * a + 128], T.UQ[:], T.US[:], True, True))
+
+    def score_row(b):
+        need("t", huq, hq[2 * b], hq[2 * b + 1])
+        hsb[b] = one(te.matmul_mx(T["SB%d" % b][:, 0:256], T.UQ[:], T.US[:], T.XQ[:, 256 * b:256 * b + 256],
+                                  T.XS[:, 256 * b:256 * b + 256], True, True))
+
+    hc = [ev() for a in range(4)]
+    heq = [None] * 4
+
+    def compare(a, k0, k1, op):
+        b = k0 // 256
+        need("v", hsb[b], hsc[a])
+        inc(hc[a], v.tensor_scalar(T.C[:, 640 * a + 128 + k0:640 * a + 128 + k1],
+                                   T["SB%d" % b][:, k0 - 256 * b:k1 - 256 * b], T["SC%d" % a][:, 0:1], None, op))
+
+    def equals(a):
+        b, k = a // 2, 128 * (a % 2)
+        need("v", hsb[b], hsc[a])
+        heq[a] = one(v.tensor_scalar(T.EQ[:, 128 * a:128 * a + 128], T["SB%d" % b][:, k:k + 128],
+                                     T["SC%d" % a][:, 0:1], -1.0, eq, mult))
+
+    def late_equals(a):
+        need("v", heq[a], hmk)
+        inc(hc[a], v.tensor_tensor_scan(T.C[:, 640 * a:640 * a + 128], T.EQ[:, 128 * a:128 * a + 128], T.MK[:],
+                                        0.0, add, mult))
+
+    hcnt = [None] * 4
+
+    def total(a):
+        need("s", hc[a])
+        hcnt[a] = one(s.activation(T.JK[:, 520 * a:520 * a + 513], T.C[:, 640 * a + 127:640 * a + 640], Copy,
+                                   accum_out=T.CNT[:, 258 - a:259 - a]))
+
+    quant_x(0); score_col(0)
+    quant_x(1); score_col(1); score_row(0)
+    quant_x(2); score_col(2)
+    equals(0); compare(0, 0, 128, ge); compare(0, 128, 256, gt)
+    quant_x(3); score_row(1); score_col(3)
+    equals(1); late_equals(0); compare(1, 0, 256, ge); late_equals(1)
+    compare(0, 256, 512, gt); total(0)
+    compare(1, 256, 512, gt); total(1)
+    equals(2); compare(2, 0, 256, ge); compare(2, 256, 384, ge); late_equals(2); compare(2, 384, 512, gt); total(2)
+    equals(3); compare(3, 0, 256, ge); late_equals(3); compare(3, 256, 512, ge)
+
+    hxm, hof = ev(), ev()
+
+    def round16(i, c):
+        h = ev()
+        inc(h, v.tensor_scalar(T.XM[:, i:i + 2], T.CNT[:, c:c + 2], -7.5, MAGIC, add, add))
+        inc(h, v.tensor_scalar(T.XM[:, i + 4:i + 6], T.CNT[:, c:c + 2], 8.5, MAGIC, add, add))
+        return h
+
+    def offset(i, c, a):
+        inc(hof, v.tensor_scalar(T.OF[:, 2 * a:2 * a + 2], T.XM[:, i:8:4], MAGIC, T.CNT[:, c:c + 1], sub, add))
+
+    need("v", hcnt[0], hcnt[1])
+    h01 = round16(0, 257)
+    need("v", hc[3])
+    hcnt[3] = one(v.tensor_tensor_scan(T.CNT[:, 0:256], T.C[:, 2048:2304], T.C[:, 2304:2560], T.C[:, 2047:2048], add, add))
+    need("v", h01)
+    offset(0, 257, 1); offset(1, 258, 0)
+    need("v", hcnt[2], hcnt[3])
+    h23 = round16(2, 255)
+    need("v", h23)
+    offset(2, 255, 3); offset(3, 256, 2)
+
+    need("v", hof, hsw, hj)
+    h = one(v.tensor_copy(T.SW[:, 0:1024].indirect(T.OF[:, 0:8]), T.J[:]))
+    need("v", h)
+    h = one(v.transpose(T.TT[:], T.SW[:]))
+    need("v", h)
+    hz = one(v.tensor_tensor(T.Z[:, 0:32], T.TT[:, 0:1024:32], T.TT[:, 16:1024:32], add))
+    hzd = ev()
+    need("y", hz)
+    need("s", hz)
+    for k in (1, 2, 3):
+        m = 32 * k
+        inc(hzd, sy.dma_start(T.Z[0:128 - m, m:m + 32], T.Z[m:128, 0:32]), 16)
+        inc(hzd, s.dma_start(T.Z[128 - m:128, m:m + 32], T.Z[0:m, 0:32]), 16)
+    need("v", hw)
+    hwq = one(v.quantize_mx(T.WQ[:], T.WS[:], T.WB[:]))
+    need("v", hzd)
+    h = one(v.tensor_tensor(T.HA[:], T.Z[:, 0:64], T.Z[:, 64:128], add))
+    need("v", h)
+    hhb = one(v.tensor_tensor(T.HB[:], T.HA[:, 0:32], T.HA[:, 32:64], add))
+    need("v", hhb)
+    hot = [None] * 4
+    for e in (2, 0, 3, 1):
+        hot[e] = one(v.tensor_scalar(T["OT%d" % e][:], T.HB[:], 4.0, 1024.0 + e, mult, add))
+
+    hg = [ev(), ev()]
+    hgq = [None, None]
+
+    def gather(q, half, e):
+        need(q, hot[e])
+        out = T.G[:, 1024 * half + e:1024 * half + 1024:4]
+        win = T.XB[:, 0:2048].indirect(T["OT%d" % e][:, 16 * half:16 * half + 16])
+        return v.tensor_copy(out, win) if q == "v" else s.activation(out, win, Copy)
+
+    def gather_half(half):
+        hv, hs = ev(), ev()
+        for e in (0, 1):
+            inc(hv, gather("v", half, e))
+        for e in (2, 3):
+            inc(hs, gather("s", half, e))
+        need("v", hv, hs)
+        hgq[half] = one(v.quantize_mx(T.GQ[:, 256 * half:256 * half + 256], T.GS[:, 256 * half:256 * half + 256],
+                                      T.G[:, 1024 * half:1024 * half + 1024]))
+
+    own = r // 4
+    oth = 1 - own
+    gather_half(oth)
+    hiv = one(v.transpose(T.IV[:], T.HB[:]))
+    gather_half(own)
+    need("v", hiv)
+    hif = one(v.tensor_scalar(T.IF[:], T.IV[:], 256.0, None, add))
+
+    nsent = [0]
+
+    def fused(parts, sem):
+        ts = []
+        for d, eng, src, dst in parts:
+            rid, pid, _se = topo.addr(T.cores[d])
+            ts.append(RemoteDMATransfer(dst_ids=[DstId(rid=rid, pnc=pid)], dma_engine_mask=sum(1 << e for e in eng),
+                                        remote_sem=sem, src=src, dst=dst))
+            nsent[0] += len(eng)
+        g.remote_dma_fused(ts, local_sem=T.sem.sent)
+
+    def codes(buf, c):
+        return buf[:, c:c + CH].bitcast(dt_u8)
+
+    dt_u8 = T.XS.dtype
+    need("g", hgq[oth])
+    far = [r ^ k for k in (7, 5, 6, 4)]
+    la = CH * (r % 4)
+    pc, ps = [], []
+    for i, d in enumerate(far):
+        e = topo.engines(core, T.cores[d])
+        w = len(e) // 4
+        pc.append((d, e[w * i:w * i + w], codes(T.GQ, CH * d), codes(T.LAQ, la)))
+        ps.append((d, e[w * i:w * i + w], T.GS[:, CH * d:CH * d + CH], T.LAS[:, la:la + CH]))
+    fused(pc, T.sem.arrA)
+    fused(ps, T.sem.arrA)
+    need("g", hgq[own])
+    near = [r ^ k for k in (3, 1, 2)]
+    pc, ps = [], []
+    for i, d in enumerate(near):
+        e = topo.engines(core, T.cores[d])
+        w = len(e) // 4
+        cut = [e[0:w], e[w:2 * w], e[2 * w:]]
+        alt = [e[2 * w:3 * w], e[3 * w:], e[0:2 * w]]
+        slot = CH * ((r % 4) - (1 if r % 4 > d % 4 else 0))
+        pc.append((d, cut[i], codes(T.GQ, CH * d), codes(T.LBQ, slot)))
+        ps.append((d, alt[i], T.GS[:, CH * d:CH * d + CH], T.LBS[:, slot:slot + CH]))
+    fused(pc, T.sem.arrB)
+    fused(ps, T.sem.arrB)
+
+    need("y", hif)
+    hid = ev()
+    inc(hid, sy.dma_start(T.IXD[:, 0:64, 0], T.IF[0:32, 0:16]), 16)
+    inc(hid, sy.dma_start(T.IXD[:, 64:128, 0], T.IF[0:32, 16:32]), 16)
+    hio = one(sy.dma_start(T.ix[r:r + 1, :], T.IF[4 * r:4 * r + 4, 0:16]), 16)
+    need("g", hid)
+    fused([(d, topo.engines(core, T.cores[d])[i:i + 1], T.IXD[d], T.IXL[r]) for i, d in enumerate(far + near)], T.sem.arrX)
+
+    def product(bank, o, q, sc):
+        return te.matmul_mx(bank, T.WQ[:, 128 * o:128 * o + 128], T.WS[:, 128 * o:128 * o + 128], q, sc, True, True)
+
+    def take(src, o, c, bank, h):
+        out = T.Y[:, (2 * src + o) * CH:(2 * src + o) * CH + CH]
+        inp = bank[:, c:c + CH]
+        inc(h, v.tensor_copy(out, inp) if o == 0 else s.activation(out, inp, Copy))
+
+    def finish(srcs, cols, banks, q, sc, n):
+        hp = [one(product(banks[o][:, 0:n], o, q, sc)) for o in range(O)]
+        hv, hs = ev(), ev()
+        need("v", hp[0])
+        need("s", hp[1])
+        for src, c in zip(srcs, cols):
+            take(src, 0, c, banks[0], hv)
+            take(src, 1, c, banks[1], hs)
+        return hv, hs
+
+    hy = ev()
+    need("t", hwq, hgq[own])
+    p0 = CH * (r - r % 2)
+    hv, hs = finish([r], [CH * (r % 2)], (T.SB0, T.SB1), T.GQ[:, p0:p0 + 128], T.GS[:, p0:p0 + 128], 128)
+    need("y", hv, hs)
+    hy0 = one(sy.dma_start(T.y[:, 128 * r:128 * r + 128], T.Y[:, 128 * r:128 * r + 128]), 16)
+
+    te.wait_ge(T.sem.arrA, 16)
+    hv, hs = finish([4 * oth + i for i in range(4)], [CH * i for i in range(4)], (T.SC0, T.SC1), T.LAQ[:], T.LAS[:], 256)
+    need("y", hv, hs)
+    hy1 = one(sy.dma_start(T.y[:, 512 * oth:512 * oth + 512], T.Y[:, 512 * oth:512 * oth + 512]), 16)
+
+    te.wait_ge(T.sem.arrB, 16)
+    rest = [4 * own + i for i in range(4) if 4 * own + i != r]
+    hv, hs = finish(rest, [CH * i for i in range(3)], (T.SC2, T.SC3), T.LBQ[:], T.LBS[:], 192)
+    lo, hi = (512 * own, 128 * r), (128 * r + 128, 512 * own + 512)
+    need("y", hv, hs)
+    if lo[0] < lo[1]:
+        inc(hy, sy.dma_start(T.y[:, lo[0]:lo[1]], T.Y[:, lo[0]:lo[1]]), 16)
+    if hi[0] < hi[1]:
+        need("s", hv, hs)
+        inc(hy, s.dma_start(T.y[:, hi[0]:hi[1]], T.Y[:, hi[0]:hi[1]]), 16)
+    s.wait_ge(T.sem.arrX, 7)
+    for a, b in ((0, r), (r + 1, N)):
+        if a < b:
+            inc(hy, s.dma_start(T.ix[a:b, :], T.IXL[a:b, 0:64, 0]), 16)
+
+    g.wait_ge(T.sem.sent, nsent[0])
+    for h in events:
+        if h[0] not in done and h[1]:
+            need("g", h)

@@ -23,8 +23,8 @@ SCRATCH = {
     "XM": ("sbuf", [128, 8], "float32"), "OF": ("sbuf", [128, 8], "uint16"),
     "SW": ("sbuf", [128, 1024], "bfloat16"), "TT": ("sbuf", [128, 1024], "bfloat16"),
     "Z": ("sbuf", [128, 128], "bfloat16"), "HA": ("sbuf", [128, 64], "bfloat16"), "HB": ("sbuf", [128, 32], "bfloat16"),
-    "OT0": ("sbuf", [128, 32], "uint16"), "OT1": ("sbuf", [128, 32], "uint16"),
-    "OT2": ("sbuf", [128, 32], "uint16"), "OT3": ("sbuf", [128, 32], "uint16"),
+    "OT": ("sbuf", [128, 32], "uint16"),
+    "PL": ("sbuf", [128, 2048], "bfloat16"),
     "G": ("sbuf", [128, 2048], "bfloat16"),
     "GQ": ("sbuf", [128, 512], MX4), "GS": ("sbuf", [128, 512], "uint8"),
     "LAQ": ("sbuf", [128, 256], MX4), "LAS": ("sbuf", [128, 256], "uint8"),
@@ -77,6 +77,7 @@ def rank_program(g, core, T, topo):
     for a in range(4):
         q = s if a % 2 == 0 else sy
         hx[a] = one(q.dma_start(T.XB[:, 512 * a:512 * a + 512], T.x[:, 512 * a:512 * a + 512]), 16)
+    need("y", *hx)
     hw = one(sy.dma_start(T.WB[:], T.w[:]), 16)
 
     hpi = one(g.iota(T.PI[:], [[0, 32]], 0, 1))
@@ -91,15 +92,16 @@ def rank_program(g, core, T, topo):
     huo = one(v.tensor_copy(T.UO[:], T.UI[:]))
     need("v", hgi)
     hgf = one(v.tensor_copy(T.GF[:, 0:1], T.GI[:, 0:1]))
-    need("v", huo, hu)
-    hur = one(v.tensor_copy(T.UR[:], T.UB[:, 0:16].indirect(T.UO[:, 0:32])))
+    hsw = one(v.memset(T.SW[:], 0.0))
     need("v", hgf, hjf)
     hj = one(v.tensor_scalar(T.J[:], T.JF[:], T.GF[:, 0:1], None, add))
-    need("v", hur)
-    huq = one(v.quantize_mx(T.UQ[:], T.US[:], T.UR[:]))
-    hsw = one(v.memset(T.SW[:], 0.0))
+    need("s", huo, hu)
+    hur1 = one(s.activation(T.UR[:, 256:512], T.UB[:, 0:16].indirect(T.UO[:, 16:32]), Copy))
+    need("v", huo, hu)
+    hur0 = one(v.tensor_copy(T.UR[:, 0:256], T.UB[:, 0:16].indirect(T.UO[:, 0:16])))
 
     hq, hsc, hsb = [None] * 4, [None] * 4, [None] * 2
+    huq = ev()
 
     def quant_x(a):
         need("v", hx[a])
@@ -143,8 +145,19 @@ def rank_program(g, core, T, topo):
         hcnt[a] = one(s.activation(T.JK[:, 520 * a:520 * a + 513], T.C[:, 640 * a + 127:640 * a + 640], Copy,
                                    accum_out=T.CNT[:, 258 - a:259 - a]))
 
-    quant_x(0); score_col(0)
-    quant_x(1); score_col(1); score_row(0)
+    hpl = [None] * 4
+
+    def plane(q, e):
+        need(q, *hx)
+        out, inp = T.PL[:, 512 * e:512 * e + 512], T.XB[:, e:2048:4]
+        hpl[e] = one(v.tensor_copy(out, inp) if q == "v" else s.activation(out, inp, Copy))
+
+    plane("s", 2); plane("s", 3)
+    quant_x(0)
+    need("v", hur0, hur1)
+    inc(huq, v.quantize_mx(T.UQ[:], T.US[:], T.UR[:]))
+    score_col(0)
+    quant_x(1); score_row(0); score_col(1)
     quant_x(2); score_col(2)
     equals(0); compare(0, 0, 128, ge); compare(0, 128, 256, gt)
     quant_x(3); score_row(1); score_col(3)
@@ -154,7 +167,7 @@ def rank_program(g, core, T, topo):
     equals(2); compare(2, 0, 256, ge); compare(2, 256, 384, ge); late_equals(2); compare(2, 384, 512, gt); total(2)
     equals(3); compare(3, 0, 256, ge); late_equals(3); compare(3, 256, 512, ge)
 
-    hxm, hof = ev(), ev()
+    hof = ev()
 
     def round16(i, c):
         h = ev()
@@ -189,45 +202,48 @@ def rank_program(g, core, T, topo):
         m = 32 * k
         inc(hzd, sy.dma_start(T.Z[0:128 - m, m:m + 32], T.Z[m:128, 0:32]), 16)
         inc(hzd, s.dma_start(T.Z[128 - m:128, m:m + 32], T.Z[0:m, 0:32]), 16)
-    need("v", hw)
-    hwq = one(v.quantize_mx(T.WQ[:], T.WS[:], T.WB[:]))
+    plane("v", 0); plane("v", 1)
     need("v", hzd)
     h = one(v.tensor_tensor(T.HA[:], T.Z[:, 0:64], T.Z[:, 64:128], add))
     need("v", h)
     hhb = one(v.tensor_tensor(T.HB[:], T.HA[:, 0:32], T.HA[:, 32:64], add))
     need("v", hhb)
-    hot = [None] * 4
-    for e in (2, 0, 3, 1):
-        hot[e] = one(v.tensor_scalar(T["OT%d" % e][:], T.HB[:], 4.0, 1024.0 + e, mult, add))
+    hot = one(v.tensor_scalar(T.OT[:], T.HB[:], 256.0, None, add))
 
-    hg = [ev(), ev()]
-    hgq = [None, None]
-
-    def gather(q, half, e):
-        need(q, hot[e])
-        out = T.G[:, 1024 * half + e:1024 * half + 1024:4]
-        win = T.XB[:, 0:2048].indirect(T["OT%d" % e][:, 16 * half:16 * half + 16])
+    def gather(q, run, n, e):
+        need(q, hot, hpl[e])
+        out = T.G[:, 256 * run + e:256 * (run + n):4]
+        win = T.PL[:, 512 * e:512 * e + 512].indirect(T.OT[:, 4 * run:4 * (run + n)])
         return v.tensor_copy(out, win) if q == "v" else s.activation(out, win, Copy)
 
-    def gather_half(half):
+    def gather_runs(run, n):
         hv, hs = ev(), ev()
         for e in (0, 1):
-            inc(hv, gather("v", half, e))
+            inc(hv, gather("v", run, n, e))
         for e in (2, 3):
-            inc(hs, gather("s", half, e))
+            inc(hs, gather("s", run, n, e))
+        return hv, hs
+
+    def quant_runs(run, n, hv, hs):
         need("v", hv, hs)
-        hgq[half] = one(v.quantize_mx(T.GQ[:, 256 * half:256 * half + 256], T.GS[:, 256 * half:256 * half + 256],
-                                      T.G[:, 1024 * half:1024 * half + 1024]))
+        return one(v.quantize_mx(T.GQ[:, CH * run:CH * (run + n)], T.GS[:, CH * run:CH * (run + n)],
+                                 T.G[:, 256 * run:256 * (run + n)]))
 
     own = r // 4
     oth = 1 - own
-    gather_half(oth)
+    first, second = 2 * ((r // 2) ^ 3), 2 * ((r // 2) ^ 2)
+    hv, hs = gather_runs(first, 2)
     hiv = one(v.transpose(T.IV[:], T.HB[:]))
-    gather_half(own)
+    hq1 = quant_runs(first, 2, hv, hs)
     need("v", hiv)
     hif = one(v.tensor_scalar(T.IF[:], T.IV[:], 256.0, None, add))
+    hq2 = quant_runs(second, 2, *gather_runs(second, 2))
+    hq3 = quant_runs(4 * own, 4, *gather_runs(4 * own, 4))
+    need("v", hw)
+    hwq = one(v.quantize_mx(T.WQ[:], T.WS[:], T.WB[:]))
 
     nsent = [0]
+    dt_u8 = T.XS.dtype
 
     def fused(parts, sem):
         ts = []
@@ -241,19 +257,23 @@ def rank_program(g, core, T, topo):
     def codes(buf, c):
         return buf[:, c:c + CH].bitcast(dt_u8)
 
-    dt_u8 = T.XS.dtype
-    need("g", hgq[oth])
-    far = [r ^ k for k in (7, 5, 6, 4)]
     la = CH * (r % 4)
-    pc, ps = [], []
-    for i, d in enumerate(far):
-        e = topo.engines(core, T.cores[d])
-        w = len(e) // 4
-        pc.append((d, e[w * i:w * i + w], codes(T.GQ, CH * d), codes(T.LAQ, la)))
-        ps.append((d, e[w * i:w * i + w], T.GS[:, CH * d:CH * d + CH], T.LAS[:, la:la + CH]))
-    fused(pc, T.sem.arrA)
+    ps, far = [], []
+    for hqk, pair in ((hq1, first), (hq2, second)):
+        need("g", hqk)
+        pc = []
+        for i in range(2):
+            d = pair + i
+            e = topo.engines(core, T.cores[d])
+            w = len(e) // 2
+            pc.append((d, e[w * i:w * i + w], codes(T.GQ, CH * d), codes(T.LAQ, la)))
+            w = len(e) // 4
+            j = len(ps)
+            ps.append((d, e[w * j:w * j + w], T.GS[:, CH * d:CH * d + CH], T.LAS[:, la:la + CH]))
+            far.append(d)
+        fused(pc, T.sem.arrA)
     fused(ps, T.sem.arrA)
-    need("g", hgq[own])
+    need("g", hq3)
     near = [r ^ k for k in (3, 1, 2)]
     pc, ps = [], []
     for i, d in enumerate(near):
@@ -271,7 +291,7 @@ def rank_program(g, core, T, topo):
     hid = ev()
     inc(hid, sy.dma_start(T.IXD[:, 0:64, 0], T.IF[0:32, 0:16]), 16)
     inc(hid, sy.dma_start(T.IXD[:, 64:128, 0], T.IF[0:32, 16:32]), 16)
-    hio = one(sy.dma_start(T.ix[r:r + 1, :], T.IF[4 * r:4 * r + 4, 0:16]), 16)
+    one(sy.dma_start(T.ix[r:r + 1, :], T.IF[4 * r:4 * r + 4, 0:16]), 16)
     need("g", hid)
     fused([(d, topo.engines(core, T.cores[d])[i:i + 1], T.IXD[d], T.IXL[r]) for i, d in enumerate(far + near)], T.sem.arrX)
 
@@ -294,16 +314,16 @@ def rank_program(g, core, T, topo):
         return hv, hs
 
     hy = ev()
-    need("t", hwq, hgq[own])
+    need("t", hwq, hq3)
     p0 = CH * (r - r % 2)
     hv, hs = finish([r], [CH * (r % 2)], (T.SB0, T.SB1), T.GQ[:, p0:p0 + 128], T.GS[:, p0:p0 + 128], 128)
     need("y", hv, hs)
-    hy0 = one(sy.dma_start(T.y[:, 128 * r:128 * r + 128], T.Y[:, 128 * r:128 * r + 128]), 16)
+    one(sy.dma_start(T.y[:, 128 * r:128 * r + 128], T.Y[:, 128 * r:128 * r + 128]), 16)
 
-    te.wait_ge(T.sem.arrA, 16)
+    te.wait_ge(T.sem.arrA, 24)
     hv, hs = finish([4 * oth + i for i in range(4)], [CH * i for i in range(4)], (T.SC0, T.SC1), T.LAQ[:], T.LAS[:], 256)
     need("y", hv, hs)
-    hy1 = one(sy.dma_start(T.y[:, 512 * oth:512 * oth + 512], T.Y[:, 512 * oth:512 * oth + 512]), 16)
+    one(sy.dma_start(T.y[:, 512 * oth:512 * oth + 512], T.Y[:, 512 * oth:512 * oth + 512]), 16)
 
     te.wait_ge(T.sem.arrB, 16)
     rest = [4 * own + i for i in range(4) if 4 * own + i != r]

from concourse.bass import DstId, RemoteDMATransfer
from concourse.mybir import AluOpType, ActivationFunctionType

N, TC, O, CH = 8, 512, 2, 64
MX4 = "float8_e4m3fn_x4"
SCRATCH = {
    "UB": ("sbuf", [128, 16], "bfloat16"),
    "UR": ("sbuf", [128, 512], "bfloat16"),
    "UQ": ("sbuf", [128, 128], MX4), "US": ("sbuf", [128, 128], "uint8"),
    "XB": ("sbuf", [128, 2048], "bfloat16"),
    "XQ": ("sbuf", [128, 512], MX4), "XS": ("sbuf", [128, 512], "uint8"),
    "WB": ("sbuf", [128, 1024], "bfloat16"),
    "WQ": ("sbuf", [128, 256], MX4), "WS": ("sbuf", [128, 256], "uint8"),
    "PI": ("sbuf", [128, 32], "int32"),
    "UI": ("sbuf", [128, 32], "int32"), "UO": ("sbuf", [128, 32], "uint16"),
    "GI": ("sbuf", [128, 8], "int32"), "GF": ("sbuf", [128, 8], "float32"),
    "JF": ("sbuf", [128, 128], "float32"), "J": ("sbuf", [128, 128], "bfloat16"),
    "ONE": ("sbuf", [128, 128], "bfloat16"), "MK": ("sbuf", [128, 128], "bfloat16"),
    "C": ("sbuf", [128, 2560], "bfloat16"),
    "EQ": ("sbuf", [128, 512], "bfloat16"),
    "JK": ("sbuf", [128, 1560], "bfloat16"),
    "CNT": ("sbuf", [128, 264], "float32"),
    "XM": ("sbuf", [128, 8], "float32"), "OF": ("sbuf", [128, 8], "uint16"),
    "SW": ("sbuf", [128, 1024], "bfloat16"), "TT": ("sbuf", [128, 1024], "bfloat16"),
    "Z": ("sbuf", [128, 128], "bfloat16"), "HA": ("sbuf", [128, 64], "bfloat16"), "HB": ("sbuf", [128, 32], "bfloat16"),
    "OT": ("sbuf", [128, 32], "uint16"),
    "PL": ("sbuf", [128, 2048], "bfloat16"),
    "G": ("sbuf", [128, 2048], "bfloat16"),
    "GQ": ("sbuf", [128, 512], MX4), "GS": ("sbuf", [128, 512], "uint8"),
    "LAQ": ("sbuf", [128, 256], MX4), "LAS": ("sbuf", [128, 256], "uint8"),
    "LBQ": ("sbuf", [128, 192], MX4), "LBS": ("sbuf", [128, 192], "uint8"),
    "IV": ("sbuf", [128, 32], "bfloat16"), "IF": ("sbuf", [128, 32], "float32"),
    "IXD": ("dram", [8, 128, 1], "float32"), "IXL": ("dram", [8, 128, 1], "float32"),
    "Y": ("sbuf", [128, 1024], "float32"),
    "SB0": ("psum", [128, 512], "float32"), "SB1": ("psum", [128, 512], "float32"),
    "SC0": ("psum", [128, 512], "float32"), "SC1": ("psum", [128, 512], "float32"),
    "SC2": ("psum", [128, 512], "float32"), "SC3": ("psum", [128, 512], "float32"),
}
NEV = 100
SEMAPHORES = ["arrA", "arrB", "arrX", "sent"] + ["e%d" % i for i in range(NEV)]
MAGIC = 1.5 * 2.0 ** 27


def rank_program(g, core, T, topo):
    r = T.rank_of(core)
    if r is None:
        return
    add, sub, mult = AluOpType.add, AluOpType.subtract, AluOpType.mult
    ge, gt, eq = AluOpType.is_ge, AluOpType.is_gt, AluOpType.is_equal
    Copy = ActivationFunctionType.Copy
    v, s, te, sy = g.vector, g.scalar, g.tensor, g.sync
    Q = {"g": g, "v": v, "s": s, "t": te, "y": sy}
    events, seen, done = [], set(), set()

    def ev():
        h = [len(events), 0]
        events.append(h)
        return h

    def inc(h, ins, n=1):
        ins.then_inc(T.sem["e%d" % h[0]], n)
        h[1] += n
        return h

    def one(ins, n=1):
        return inc(ev(), ins, n)

    def need(q, *hs):
        for h in hs:
            if (q, h[0]) not in seen:
                seen.add((q, h[0]))
                done.add(h[0])
                Q[q].wait_ge(T.sem["e%d" % h[0]], h[1])

    hx = [None] * 4
    hu = one(sy.dma_start(T.UB[:], T.u[:, 0:16]), 16)
    for a in range(4):
        q = s if a % 2 == 0 else sy
        hx[a] = one(q.dma_start(T.XB[:, 512 * a:512 * a + 512], T.x[:, 512 * a:512 * a + 512]), 16)
    need("y", *hx)
    hw = one(sy.dma_start(T.WB[:], T.w[:]), 16)

    hpi = one(g.iota(T.PI[:], [[0, 32]], 0, 1))
    hjf = one(g.iota(T.JF[:], [[128, 4], [0, 2], [1, 16]], -256, 0, allow_small_or_imprecise_dtypes=True))
    hone = one(v.memset(T.ONE[:], 1.0))
    need("g", hone)
    hmk = one(g.affine_select(T.MK[:], T.ONE[:], [[1, 128]], ge, 0.0, 0, -1))
    need("v", hpi)
    hui = one(v.tensor_scalar(T.UI[:], T.PI[:], 3, None, AluOpType.bitwise_and))
    hgi = one(v.tensor_scalar(T.GI[:, 0:1], T.PI[:, 0:1], 112, None, AluOpType.bitwise_and))
    need("v", hui)
    huo = one(v.tensor_copy(T.UO[:], T.UI[:]))
    need("v", hgi)
    hgf = one(v.tensor_copy(T.GF[:, 0:1], T.GI[:, 0:1]))
    hsw = one(v.memset(T.SW[:], 0.0))
    need("v", hgf, hjf)
    hj = one(v.tensor_scalar(T.J[:], T.JF[:], T.GF[:, 0:1], None, add))
    need("s", huo, hu)
    hur1 = one(s.activation(T.UR[:, 256:512], T.UB[:, 0:16].indirect(T.UO[:, 16:32]), Copy))
    need("v", huo, hu)
    hur0 = one(v.tensor_copy(T.UR[:, 0:256], T.UB[:, 0:16].indirect(T.UO[:, 0:16])))

    hq, hsc, hsb = [None] * 4, [None] * 4, [None] * 2
    huq = ev()

    def quant_x(a):
        need("v", hx[a])
        hq[a] = one(v.quantize_mx(T.XQ[:, 128 * a:128 * a + 128], T.XS[:, 128 * a:128 * a + 128],
                                  T.XB[:, 512 * a:512 * a + 512]))

    def score_col(a):
        need("t", huq, hq[a])
        hsc[a] = one(te.matmul_mx(T["SC%d" % a][:, 0:128], T.XQ[:, 128 * a:128 * a + 128],
                                  T.XS[:, 128 * a:128 * a + 128], T.UQ[:], T.US[:], True, True))

    def score_row(b):
        need("t", huq, hq[2 * b], hq[2 * b + 1])
        hsb[b] = one(te.matmul_mx(T["SB%d" % b][:, 0:256], T.UQ[:], T.US[:], T.XQ[:, 256 * b:256 * b + 256],
                                  T.XS[:, 256 * b:256 * b + 256], True, True))

    hc = [ev() for a in range(4)]
    heq = [None] * 4

    def compare(a, k0, k1, op):
        b = k0 // 256
        need("v", hsb[b], hsc[a])
        inc(hc[a], v.tensor_scalar(T.C[:, 640 * a + 128 + k0:640 * a + 128 + k1],
                                   T["SB%d" % b][:, k0 - 256 * b:k1 - 256 * b], T["SC%d" % a][:, 0:1], None, op))

    def equals(a):
        b, k = a // 2, 128 * (a % 2)
        need("v", hsb[b], hsc[a])
        heq[a] = one(v.tensor_scalar(T.EQ[:, 128 * a:128 * a + 128], T["SB%d" % b][:, k:k + 128],
                                     T["SC%d" % a][:, 0:1], -1.0, eq, mult))

    def late_equals(a):
        need("v", heq[a], hmk)
        inc(hc[a], v.tensor_tensor_scan(T.C[:, 640 * a:640 * a + 128], T.EQ[:, 128 * a:128 * a + 128], T.MK[:],
                                        0.0, add, mult))

    hcnt = [None] * 4

    def total(a):
        need("s", hc[a])
        hcnt[a] = one(s.activation(T.JK[:, 520 * a:520 * a + 513], T.C[:, 640 * a + 127:640 * a + 640], Copy,
                                   accum_out=T.CNT[:, 258 - a:259 - a]))

    hpl = [None] * 4

    def plane(q, e):
        need(q, *hx)
        out, inp = T.PL[:, 512 * e:512 * e + 512], T.XB[:, e:2048:4]
        hpl[e] = one(v.tensor_copy(out, inp) if q == "v" else s.activation(out, inp, Copy))

    plane("s", 2); plane("s", 3)
    quant_x(0)
    need("v", hur0, hur1)
    inc(huq, v.quantize_mx(T.UQ[:], T.US[:], T.UR[:]))
    score_col(0)
    quant_x(1); score_row(0); score_col(1)
    quant_x(2); score_col(2)
    equals(0); compare(0, 0, 128, ge); compare(0, 128, 256, gt)
    quant_x(3); score_row(1); score_col(3)
    equals(1); late_equals(0); compare(1, 0, 256, ge); late_equals(1)
    compare(0, 256, 512, gt); total(0)
    compare(1, 256, 512, gt); total(1)
    equals(2); compare(2, 0, 256, ge); compare(2, 256, 384, ge); late_equals(2); compare(2, 384, 512, gt); total(2)
    equals(3); compare(3, 0, 256, ge); late_equals(3); compare(3, 256, 512, ge)

    hof = ev()

    def round16(i, c):
        h = ev()
        inc(h, v.tensor_scalar(T.XM[:, i:i + 2], T.CNT[:, c:c + 2], -7.5, MAGIC, add, add))
        inc(h, v.tensor_scalar(T.XM[:, i + 4:i + 6], T.CNT[:, c:c + 2], 8.5, MAGIC, add, add))
        return h

    def offset(i, c, a):
        inc(hof, v.tensor_scalar(T.OF[:, 2 * a:2 * a + 2], T.XM[:, i:8:4], MAGIC, T.CNT[:, c:c + 1], sub, add))

    need("v", hcnt[0], hcnt[1])
    h01 = round16(0, 257)
    need("v", hc[3])
    hcnt[3] = one(v.tensor_tensor_scan(T.CNT[:, 0:256], T.C[:, 2048:2304], T.C[:, 2304:2560], T.C[:, 2047:2048], add, add))
    need("v", h01)
    offset(0, 257, 1); offset(1, 258, 0)
    need("v", hcnt[2], hcnt[3])
    h23 = round16(2, 255)
    need("v", h23)
    offset(2, 255, 3); offset(3, 256, 2)

    need("v", hof, hsw, hj)
    h = one(v.tensor_copy(T.SW[:, 0:1024].indirect(T.OF[:, 0:8]), T.J[:]))
    need("v", h)
    h = one(v.transpose(T.TT[:], T.SW[:]))
    need("v", h)
    hz = one(v.tensor_tensor(T.Z[:, 0:32], T.TT[:, 0:1024:32], T.TT[:, 16:1024:32], add))
    hzd = ev()
    need("y", hz)
    need("s", hz)
    for k in (1, 2, 3):
        m = 32 * k
        inc(hzd, sy.dma_start(T.Z[0:128 - m, m:m + 32], T.Z[m:128, 0:32]), 16)
        inc(hzd, s.dma_start(T.Z[128 - m:128, m:m + 32], T.Z[0:m, 0:32]), 16)
    plane("v", 0); plane("v", 1)
    need("v", hzd)
    h = one(v.tensor_tensor(T.HA[:], T.Z[:, 0:64], T.Z[:, 64:128], add))
    need("v", h)
    hhb = one(v.tensor_tensor(T.HB[:], T.HA[:, 0:32], T.HA[:, 32:64], add))
    need("v", hhb)
    hot = one(v.tensor_scalar(T.OT[:], T.HB[:], 256.0, None, add))

    def gather(q, run, n, e):
        need(q, hot, hpl[e])
        out = T.G[:, 256 * run + e:256 * (run + n):4]
        win = T.PL[:, 512 * e:512 * e + 512].indirect(T.OT[:, 4 * run:4 * (run + n)])
        return v.tensor_copy(out, win) if q == "v" else s.activation(out, win, Copy)

    def gather_runs(run, n):
        hv, hs = ev(), ev()
        for e in (0, 1):
            inc(hv, gather("v", run, n, e))
        for e in (2, 3):
            inc(hs, gather("s", run, n, e))
        return hv, hs

    def quant_runs(run, n, hv, hs):
        need("v", hv, hs)
        return one(v.quantize_mx(T.GQ[:, CH * run:CH * (run + n)], T.GS[:, CH * run:CH * (run + n)],
                                 T.G[:, 256 * run:256 * (run + n)]))

    own = r // 4
    oth = 1 - own
    first, second = 2 * ((r // 2) ^ 3), 2 * ((r // 2) ^ 2)
    hv, hs = gather_runs(first, 2)
    hiv = one(v.transpose(T.IV[:], T.HB[:]))
    hq1 = quant_runs(first, 2, hv, hs)
    need("v", hiv)
    hif = one(v.tensor_scalar(T.IF[:], T.IV[:], 256.0, None, add))
    hq2 = quant_runs(second, 2, *gather_runs(second, 2))
    hq3 = quant_runs(4 * own, 4, *gather_runs(4 * own, 4))
    need("v", hw)
    hwq = one(v.quantize_mx(T.WQ[:], T.WS[:], T.WB[:]))

    nsent = [0]
    dt_u8 = T.XS.dtype

    def fused(parts, sem):
        ts = []
        for d, eng, src, dst in parts:
            rid, pid, _se = topo.addr(T.cores[d])
            ts.append(RemoteDMATransfer(dst_ids=[DstId(rid=rid, pnc=pid)], dma_engine_mask=sum(1 << e for e in eng),
                                        remote_sem=sem, src=src, dst=dst))
            nsent[0] += len(eng)
        g.remote_dma_fused(ts, local_sem=T.sem.sent)

    def codes(buf, c):
        return buf[:, c:c + CH].bitcast(dt_u8)

    la = CH * (r % 4)
    ps, far = [], []
    for hqk, pair in ((hq1, first), (hq2, second)):
        need("g", hqk)
        pc = []
        for i in range(2):
            d = pair + i
            e = topo.engines(core, T.cores[d])
            w = len(e) // 2
            pc.append((d, e[w * i:w * i + w], codes(T.GQ, CH * d), codes(T.LAQ, la)))
            w = len(e) // 4
            j = len(ps)
            ps.append((d, e[w * j:w * j + w], T.GS[:, CH * d:CH * d + CH], T.LAS[:, la:la + CH]))
            far.append(d)
        fused(pc, T.sem.arrA)
    fused(ps, T.sem.arrA)
    need("g", hq3)
    near = [r ^ k for k in (3, 1, 2)]
    pc, ps = [], []
    for i, d in enumerate(near):
        e = topo.engines(core, T.cores[d])
        w = len(e) // 4
        cut = [e[0:w], e[w:2 * w], e[2 * w:]]
        alt = [e[2 * w:3 * w], e[3 * w:], e[0:2 * w]]
        slot = CH * ((r % 4) - (1 if r % 4 > d % 4 else 0))
        pc.append((d, cut[i], codes(T.GQ, CH * d), codes(T.LBQ, slot)))
        ps.append((d, alt[i], T.GS[:, CH * d:CH * d + CH], T.LBS[:, slot:slot + CH]))
    fused(pc, T.sem.arrB)
    fused(ps, T.sem.arrB)

    need("y", hif)
    hid = ev()
    inc(hid, sy.dma_start(T.IXD[:, 0:64, 0], T.IF[0:32, 0:16]), 16)
    inc(hid, sy.dma_start(T.IXD[:, 64:128, 0], T.IF[0:32, 16:32]), 16)
    one(sy.dma_start(T.ix[r:r + 1, :], T.IF[4 * r:4 * r + 4, 0:16]), 16)
    need("g", hid)
    fused([(d, topo.engines(core, T.cores[d])[i:i + 1], T.IXD[d], T.IXL[r]) for i, d in enumerate(far + near)], T.sem.arrX)

    def product(bank, o, q, sc):
        return te.matmul_mx(bank, T.WQ[:, 128 * o:128 * o + 128], T.WS[:, 128 * o:128 * o + 128], q, sc, True, True)

    def take(src, o, c, bank, h):
        out = T.Y[:, (2 * src + o) * CH:(2 * src + o) * CH + CH]
        inp = bank[:, c:c + CH]
        inc(h, v.tensor_copy(out, inp) if o == 0 else s.activation(out, inp, Copy))

    def finish(srcs, cols, banks, q, sc, n):
        hp = [one(product(banks[o][:, 0:n], o, q, sc)) for o in range(O)]
        hv, hs = ev(), ev()
        need("v", hp[0])
        need("s", hp[1])
        for src, c in zip(srcs, cols):
            take(src, 0, c, banks[0], hv)
            take(src, 1, c, banks[1], hs)
        return hv, hs

    hy = ev()
    need("t", hwq, hq3)
    p0 = CH * (r - r % 2)
    hv, hs = finish([r], [CH * (r % 2)], (T.SB0, T.SB1), T.GQ[:, p0:p0 + 128], T.GS[:, p0:p0 + 128], 128)
    need("y", hv, hs)
    one(sy.dma_start(T.y[:, 128 * r:128 * r + 128], T.Y[:, 128 * r:128 * r + 128]), 16)

    te.wait_ge(T.sem.arrA, 24)
    hv, hs = finish([4 * oth + i for i in range(4)], [CH * i for i in range(4)], (T.SC0, T.SC1), T.LAQ[:], T.LAS[:], 256)
    need("y", hv, hs)
    one(sy.dma_start(T.y[:, 512 * oth:512 * oth + 512], T.Y[:, 512 * oth:512 * oth + 512]), 16)

    te.wait_ge(T.sem.arrB, 16)
    rest = [4 * own + i for i in range(4) if 4 * own + i != r]
    hv, hs = finish(rest, [CH * i for i in range(3)], (T.SC2, T.SC3), T.LBQ[:], T.LBS[:], 192)
    lo, hi = (512 * own, 128 * r), (128 * r + 128, 512 * own + 512)
    need("y", hv, hs)
    if lo[0] < lo[1]:
        inc(hy, sy.dma_start(T.y[:, lo[0]:lo[1]], T.Y[:, lo[0]:lo[1]]), 16)
    if hi[0] < hi[1]:
        need("s", hv, hs)
        inc(hy, s.dma_start(T.y[:, hi[0]:hi[1]], T.Y[:, hi[0]:hi[1]]), 16)
    s.wait_ge(T.sem.arrX, 7)
    for a, b in ((0, r), (r + 1, N)):
        if a < b:
            inc(hy, s.dma_start(T.ix[a:b, :], T.IXL[a:b, 0:64, 0]), 16)

    g.wait_ge(T.sem.sent, nsent[0])
    for h in events:
        if h[0] not in done and h[1]:
            need("g", h)
